import numpy as np, ml_dtypes
CORES = [7,15,23,39,47,63,71,79,87,95,119,127]
N = 12
import mx_ref
NC, WT = 128, 1
LR = np.float32(2.0 ** -3)
BF = ml_dtypes.bfloat16
def cut(t, i, w=512):
    return t[:, w * i:w * i + w]
def tile(rs):
    return np.stack(rs, axis=2).reshape(128, -1).astype(BF)
def pick(b):
    s = np.zeros((128, 128, 4), np.float32)
    s[np.arange(128), np.arange(128), b] = 1.0
    return mx_ref.quantize(s.reshape(128, 512).astype(BF))
def pk(c, s, i=0):
    return (np.ascontiguousarray(c[:, 512 * i:512 * i + 512]), mx_ref.live(s[:, 128 * i:128 * i + 128]))
def inputs(rng, e, E):
    def f(*shape):
        v = (rng.standard_normal(shape, dtype=np.float32) * np.exp2(rng.integers(-2, 3, shape[:-1] + (1,)))).astype(BF)
        return mx_ref.spread((v.astype(np.float32) * np.exp2(rng.integers(-E, E + 1, shape[:-2] + (1, 1))).astype(np.float32)).astype(BF), rng, e)
    def packed(k):
        c = np.zeros((N, 128, k * 512), np.uint8); s = np.zeros((N, 128, k * 128), np.uint8)
        for r in range(N):
            for i in range(k):
                a, b = mx_ref.quantize(f(128, 512)); c[r][:, 512 * i:512 * i + 512] = a; s[r][:, 128 * i:128 * i + 128] = mx_ref.plane(b, rng)
        return c, s
    d = {}
    d["wc"], d["ws"] = packed(WT)
    d["gr"] = f(N, 128, WT * 512)
    d["x"] = f(N, 128, 4 * NC)
    return d
def setup_inputs(rng):
    return inputs(rng, 0, 0)
def setup_inputs_blocks(rng):
    return inputs(rng, 2, 0)
def setup_inputs_wide(rng):
    return inputs(rng, 0, 4)
def setup_inputs_faint(rng):
    d = setup_inputs(rng); d["gr"] = mx_ref.flush((d["gr"].astype(np.float32) * np.float32(2.0 ** -12)).astype(BF))
    return d
def reference(wc, ws, gr, x):
    S = [pick(t) for t in range(4)]
    H = [mx_ref.quantize(tile([mx_ref.matmul(S[t], pk(wc[j], ws[j], i)) - cut(gr[j], i).astype(np.float32)[:, t::4] * LR for t in range(4)])) for j in range(N) for i in range(WT)]
    y = np.zeros((N, 128, N * WT * NC), np.float32)
    for r in range(N):
        X = mx_ref.quantize(x[r])
        for b in range(N * WT):
            y[r][:, NC * b:NC * b + NC] = mx_ref.matmul(H[b], X)
    return {"y": y}

@@ -1,0 +1,174 @@
+from concourse.bass import DstId, RemoteDMATransfer
+from concourse.mybir import dt, AluOpType, ActivationFunctionType
+
+N, NC = 12, 128
+ALL = 128
+LR = 2.0 ** -3
+
+RANK_CALLS = [("c", [1, 2, 3]), ("s", [1, 2, 3]), ("c", [4, 5]), ("s", [4, 5])]
+HELPERS = [("far", 0, [("c", [6, 7]), ("c", [8, 9]), ("c", [10, 11])]),
+           ("near", 0, [("s", [6, 7, 8]), ("s", [9, 10, 11])])]
+GROUPS = [[0, 1, 2, 3], [4, 5], [6, 7], [8, 9], [10, 11]]
+
+SCRATCH = {
+    "cw": ("sbuf", [128, NC], "float8_e4m3fn_x4"), "sw": ("sbuf", [128, NC], "uint8"),
+    "gin": ("sbuf", [128, 4 * NC], "bfloat16"), "gs": ("sbuf", [128, 4 * NC], "bfloat16"),
+    "xin": ("sbuf", [128, 4 * NC], "bfloat16"),
+    "cx": ("sbuf", [128, NC], "float8_e4m3fn_x4"), "sx": ("sbuf", [128, NC], "uint8"),
+    "one": ("sbuf", [128, 128], "bfloat16"), "eye": ("sbuf", [128, 516], "bfloat16"),
+    "cs": ("sbuf", [128, 4 * 128], "float8_e4m3fn_x4"), "ss": ("sbuf", [128, 4 * 128], "uint8"),
+    "v": ("sbuf", [128, 4 * NC], "bfloat16"),
+    "cg": ("sbuf", [128, N * NC], "float8_e4m3fn_x4"), "sg": ("sbuf", [128, N * NC], "uint8"),
+    "yb": ("sbuf", [128, N * NC], "float32"),
+    "ps": ("psum", [128, 8 * 512], "float32"),
+}
+SEMAPHORES = (["lw", "lg", "lx", "fill", "eye1", "qs", "gsc", "pd", "sub", "qv", "qx", "py", "cpv", "cpa", "st", "sent", "fed"]
+              + ["a%d" % j for j in range(N)])
+
+
+def helper_of(core, T, topo, side, k):
+    same = [c for c in range(ALL) if topo.chip(c) == topo.chip(core) and T.rank_of(c) is None
+            and (topo.die(c) == topo.die(core)) == (side == "near")
+            and all(topo.may_write(c, d) for d in T.cores)]
+    return same[k]
+
+
+def off_mask(core, T, topo):
+    return min(topo.mask(core, d) for d in T.cores if topo.chip(d) != topo.chip(core))
+
+
+def count(m):
+    return bin(m).count("1")
+
+
+def send(g, T, topo, kind, blk, dsts, mask, sem):
+    ids = []
+    for d in dsts:
+        rid, pid, _ = topo.addr(d)
+        ids.append(DstId(rid=rid, pnc=pid))
+    a, b = blk * NC, (blk + 1) * NC
+    ap = T.cg[:, a:b].bitcast(dt.uint8) if kind == "c" else T.sg[:, a:b]
+    g.remote_dma_fused([RemoteDMATransfer(dst_ids=ids, dma_engine_mask=mask, remote_sem=sem,
+                                          srcs=[ap], dsts=[ap for _ in dsts])], local_sem=T.sem.sent)
+    return count(mask)
+
+
+def helper_program(g, core, T, topo, r):
+    for side, k, calls in HELPERS:
+        if helper_of(T.cores[r], T, topo, side, k) != core:
+            continue
+        m = off_mask(core, T, topo)
+        feed = off_feed(T.cores[r], T, topo)
+        kinds = sorted({kd for kd, _ in calls})
+        g.wait_ge(T.sem.fed, count(feed) * len(kinds))
+        n = 0
+        for kd, offs in calls:
+            n += send(g, T, topo, kd, r, [T.cores[(r + d) % N] for d in offs], m, T.sem["a%d" % r])
+        g.wait_ge(T.sem.sent, n)
+
+
+def off_feed(core, T, topo):
+    here = [c for c in range(ALL) if topo.chip(c) == topo.chip(core) and c != core]
+    return topo.mask(core, here[0]) & ~off_mask(core, T, topo)
+
+
+def runs(blocks):
+    out = []
+    for b in sorted(blocks):
+        if out and out[-1][1] == b:
+            out[-1][1] = b + 1
+        else:
+            out.append([b, b + 1])
+    return out
+
+
+def rank_program(g, core, T, topo):
+    r = T.rank_of(core)
+    if r is None:
+        for j in range(N):
+            if topo.chip(T.cores[j]) == topo.chip(core):
+                helper_program(g, core, T, topo, j)
+        return
+    s = T.sem
+    v, sc, te, sy = g.vector, g.scalar, g.tensor, g.sync
+
+    sy.dma_start(T.cw[:].bitcast(dt.uint8), T.wc[:, :]).then_inc(s.lw, 16)
+    sy.dma_start(T.sw[:], T.ws[:, :]).then_inc(s.lw, 16)
+    sc.dma_start(T.gin[:], T.gr[:, :]).then_inc(s.lg, 16)
+    sy.dma_start(T.xin[:], T.x[:, :]).then_inc(s.lx, 16)
+
+    v.memset(T.one[:], 1.0).then_inc(s.fill, 1)
+    v.memset(T.eye[:], 0.0).then_inc(s.fill, 1)
+    g.wait_ge(s.fill, 2)
+    g.affine_select(T.eye[:, 3:515:4], T.one[:], [[-1, 128]], AluOpType.is_equal, 0.0, 0, 1).then_inc(s.eye1, 1)
+    v.wait_ge(s.eye1, 1)
+    for b in range(4):
+        v.quantize_mx(out=T.cs[:, 128 * b:128 * b + 128], scales=T.ss[:, 128 * b:128 * b + 128],
+                      in_=T.eye[:, 3 - b:515 - b]).then_inc(s.qs, 1)
+    v.wait_ge(s.lg, 16)
+    v.tensor_scalar(T.gs[:], T.gin[:], LR, None, AluOpType.mult).then_inc(s.gsc, 1)
+
+    te.wait_ge(s.qs, 4)
+    te.wait_ge(s.lw, 32)
+    for b in range(4):
+        te.matmul_mx(T.ps[:, 512 * b:512 * b + NC], T.cs[:, 128 * b:128 * b + 128], T.ss[:, 128 * b:128 * b + 128],
+                     T.cw[:], T.sw[:], True, True).then_inc(s.pd, 1)
+    v.wait_ge(s.gsc, 1)
+    for b in range(4):
+        v.wait_ge(s.pd, b + 1)
+        v.tensor_tensor(T.v[:, b:4 * NC:4], T.ps[:, 512 * b:512 * b + NC], T.gs[:, b:4 * NC:4],
+                        AluOpType.subtract).then_inc(s.sub, 1)
+    v.wait_ge(s.sub, 4)
+    v.quantize_mx(out=T.cg[:, NC * r:NC * r + NC], scales=T.sg[:, NC * r:NC * r + NC], in_=T.v[:]).then_inc(s.qv, 1)
+    v.wait_ge(s.lx, 16)
+    v.quantize_mx(out=T.cx[:], scales=T.sx[:], in_=T.xin[:]).then_inc(s.qx, 1)
+
+    m, feed = off_mask(core, T, topo), off_feed(core, T, topo)
+    g.wait_ge(s.qv, 1)
+    n = 0
+    for kd in ("c", "s"):
+        hs = [helper_of(core, T, topo, side, k) for side, k, calls in HELPERS if any(q == kd for q, _ in calls)]
+        if hs:
+            n += send(g, T, topo, kd, r, hs, feed, s.fed)
+    for kd, offs in RANK_CALLS:
+        n += send(g, T, topo, kd, r, [T.cores[(r + d) % N] for d in offs], m, s["a%d" % r])
+
+    per = 2 * count(m)
+
+    te.wait_ge(s.sub, 4)
+    te.wait_ge(s.qv, 1)
+    te.wait_ge(s.qx, 1)
+    order = [d for grp in GROUPS for d in grp]
+    nv, na = 0, 0
+    done = []
+    for i, d in enumerate(order):
+        b = (r - d) % N
+        if d:
+            te.wait_ge(s["a%d" % b], per)
+        if i >= 8:
+            q, k = done[i - 8]
+            te.wait_ge(q, k)
+        bank = 512 * ((4 + i) % 8)
+        te.matmul_mx(T.ps[:, bank:bank + NC], T.cg[:, NC * b:NC * b + NC], T.sg[:, NC * b:NC * b + NC],
+                     T.cx[:], T.sx[:], True, True).then_inc(s.py, 1)
+        dst, src = T.yb[:, NC * b:NC * b + NC], T.ps[:, bank:bank + NC]
+        if i % 2 == 0:
+            v.wait_ge(s.py, i + 1)
+            v.tensor_copy(dst, src).then_inc(s.cpv, 1)
+            nv += 1
+            done.append((s.cpv, nv))
+        else:
+            sc.wait_ge(s.py, i + 1)
+            sc.activation(dst, src, ActivationFunctionType.Copy).then_inc(s.cpa, 1)
+            na += 1
+            done.append((s.cpa, na))
+    i, st = 0, 0
+    for grp in GROUPS:
+        i += len(grp)
+        sy.wait_ge(s.cpv, (i + 1) // 2)
+        sy.wait_ge(s.cpa, i // 2)
+        for a, e in runs([(r - d) % N for d in grp]):
+            sy.dma_start(T.y[:, NC * a:NC * e], T.yb[:, NC * a:NC * e]).then_inc(s.st, 16)
+            st += 16
+    sy.wait_ge(s.st, st)
+    g.wait_ge(s.sent, n)

@@ -5,36 +5,57 @@ N, NC = 12, 128
 ALL = 128
 LR = 2.0 ** -3
 
-RANK_CALLS = [("c", [1, 2, 3]), ("s", [1, 2, 3]), ("c", [4, 5]), ("s", [4, 5])]
-HELPERS = [("far", 0, [("c", [6, 7]), ("c", [8, 9]), ("c", [10, 11])]),
-           ("near", 0, [("s", [6, 7, 8]), ("s", [9, 10, 11])])]
-GROUPS = [[0, 1, 2, 3], [4, 5], [6, 7], [8, 9], [10, 11]]
+HELPERS = [("far", 0, [("s", [2]), ("s", [6, 7]), ("c", [10])]),
+           ("far", 1, [("s", [10]), ("s", [9, 4]), ("c", [7]), ("c", [0]), ("c", [1])]),
+           ("near", 0, [("s", [0, 3, 1, 8]), ("c", [8]), ("c", [3])])]
+RANK_CALLS = [("feed", "s", [0, 1, 2]), ("send", "c", [6, 9, 5]), ("send", "s", [5]),
+              ("feed", "c", [0, 1]), ("feed", "c", [2]), ("send", "c", [2]), ("send", "c", [4])]
+ARRIVE = [5, 6, 9, 2, 4, 10, 7, 0, 8, 1, 3]
 
 SCRATCH = {
     "cw": ("sbuf", [128, NC], "float8_e4m3fn_x4"), "sw": ("sbuf", [128, NC], "uint8"),
-    "gin": ("sbuf", [128, 4 * NC], "bfloat16"), "gs": ("sbuf", [128, 4 * NC], "bfloat16"),
-    "xin": ("sbuf", [128, 4 * NC], "bfloat16"),
+    "gin": ("sbuf", [128, 4 * NC], "bfloat16"), "xin": ("sbuf", [128, 4 * NC], "bfloat16"),
     "cx": ("sbuf", [128, NC], "float8_e4m3fn_x4"), "sx": ("sbuf", [128, NC], "uint8"),
-    "one": ("sbuf", [128, 128], "bfloat16"), "eye": ("sbuf", [128, 516], "bfloat16"),
+    "zero": ("sbuf", [128, 128], "bfloat16"), "eye": ("sbuf", [128, 516], "bfloat16"),
     "cs": ("sbuf", [128, 4 * 128], "float8_e4m3fn_x4"), "ss": ("sbuf", [128, 4 * 128], "uint8"),
     "v": ("sbuf", [128, 4 * NC], "bfloat16"),
     "cg": ("sbuf", [128, N * NC], "float8_e4m3fn_x4"), "sg": ("sbuf", [128, N * NC], "uint8"),
     "yb": ("sbuf", [128, N * NC], "float32"),
     "ps": ("psum", [128, 8 * 512], "float32"),
 }
-SEMAPHORES = (["lw", "lg", "lx", "fill", "eye1", "qs", "gsc", "pd", "sub", "qv", "qx", "py", "cpv", "cpa", "st", "sent", "fed"]
-              + ["a%d" % j for j in range(N)])
+SEMAPHORES = (["lw", "lg", "lx", "fill", "rest", "eye1", "qs", "pd", "sub", "qv", "qx", "py", "cpv", "cpa", "st", "sent",
+               "fedc", "feds"] + ["a%d" % j for j in range(N)])
 
 
-def helper_of(core, T, topo, side, k):
+def helper_of(core, T, topo, h):
+    side, k, _ = HELPERS[h]
     same = [c for c in range(ALL) if topo.chip(c) == topo.chip(core) and T.rank_of(c) is None
             and (topo.die(c) == topo.die(core)) == (side == "near")
             and all(topo.may_write(c, d) for d in T.cores)]
     return same[k]
 
 
+def dest(r, t, T, topo):
+    ch = topo.chip(T.cores[r])
+    own = [i for i in range(N) if i == r or topo.same_plane(topo.chip(T.cores[i]), ch)]
+    other = [i for i in range(N) if i not in own]
+    at = own.index(r)
+    if t < len(own) - 1:
+        return own[(at + 1 + t) % len(own)]
+    return other[(at + t - (len(own) - 1)) % len(other)]
+
+
+def dests(r, ts, T, topo):
+    return [T.cores[dest(r, t, T, topo)] for t in ts]
+
+
 def off_mask(core, T, topo):
     return min(topo.mask(core, d) for d in T.cores if topo.chip(d) != topo.chip(core))
+
+
+def feed_mask(core, T, topo):
+    here = [c for c in range(ALL) if topo.chip(c) == topo.chip(core) and c != core]
+    return topo.mask(core, here[0]) & ~off_mask(core, T, topo)
 
 
 def count(m):
@@ -54,32 +75,17 @@ def send(g, T, topo, kind, blk, dsts, mask, sem):
 
 
 def helper_program(g, core, T, topo, r):
-    for side, k, calls in HELPERS:
-        if helper_of(T.cores[r], T, topo, side, k) != core:
+    for h in range(len(HELPERS)):
+        if helper_of(T.cores[r], T, topo, h) != core:
             continue
-        m = off_mask(core, T, topo)
-        feed = off_feed(T.cores[r], T, topo)
-        kinds = sorted({kd for kd, _ in calls})
-        g.wait_ge(T.sem.fed, count(feed) * len(kinds))
-        n = 0
-        for kd, offs in calls:
-            n += send(g, T, topo, kd, r, [T.cores[(r + d) % N] for d in offs], m, T.sem["a%d" % r])
+        m, feed = off_mask(core, T, topo), feed_mask(T.cores[r], T, topo)
+        n, seen = 0, []
+        for kd, ts in HELPERS[h][2]:
+            if kd not in seen:
+                g.wait_ge(T.sem["fed" + kd], count(feed))
+                seen.append(kd)
+            n += send(g, T, topo, kd, r, dests(r, ts, T, topo), m, T.sem["a%d" % r])
         g.wait_ge(T.sem.sent, n)
-
-
-def off_feed(core, T, topo):
-    here = [c for c in range(ALL) if topo.chip(c) == topo.chip(core) and c != core]
-    return topo.mask(core, here[0]) & ~off_mask(core, T, topo)
-
-
-def runs(blocks):
-    out = []
-    for b in sorted(blocks):
-        if out and out[-1][1] == b:
-            out[-1][1] = b + 1
-        else:
-            out.append([b, b + 1])
-    return out
 
 
 def rank_program(g, core, T, topo):
@@ -93,82 +99,70 @@ def rank_program(g, core, T, topo):
     v, sc, te, sy = g.vector, g.scalar, g.tensor, g.sync
 
     sy.dma_start(T.cw[:].bitcast(dt.uint8), T.wc[:, :]).then_inc(s.lw, 16)
-    sy.dma_start(T.sw[:], T.ws[:, :]).then_inc(s.lw, 16)
+    sc.dma_start(T.sw[:], T.ws[:, :]).then_inc(s.lw, 16)
     sc.dma_start(T.gin[:], T.gr[:, :]).then_inc(s.lg, 16)
-    sy.dma_start(T.xin[:], T.x[:, :]).then_inc(s.lx, 16)
+    sc.dma_start(T.xin[:], T.x[:, :]).then_inc(s.lx, 16)
 
-    v.memset(T.one[:], 1.0).then_inc(s.fill, 1)
-    v.memset(T.eye[:], 0.0).then_inc(s.fill, 1)
-    g.wait_ge(s.fill, 2)
-    g.affine_select(T.eye[:, 3:515:4], T.one[:], [[-1, 128]], AluOpType.is_equal, 0.0, 0, 1).then_inc(s.eye1, 1)
+    v.memset(T.zero[:], 0.0).then_inc(s.fill, 1)
+    for k in range(3):
+        v.memset(T.eye[:, k:516:4], 0.0).then_inc(s.rest, 1)
+    g.wait_ge(s.fill, 1)
+    g.affine_select(T.eye[:, 3:515:4], T.zero[:], [[-1, 128]], AluOpType.not_equal, 1.0 / LR, 0, 1).then_inc(s.eye1, 1)
+    v.wait_ge(s.rest, 3)
     v.wait_ge(s.eye1, 1)
     for b in range(4):
         v.quantize_mx(out=T.cs[:, 128 * b:128 * b + 128], scales=T.ss[:, 128 * b:128 * b + 128],
                       in_=T.eye[:, 3 - b:515 - b]).then_inc(s.qs, 1)
-    v.wait_ge(s.lg, 16)
-    v.tensor_scalar(T.gs[:], T.gin[:], LR, None, AluOpType.mult).then_inc(s.gsc, 1)
 
-    te.wait_ge(s.qs, 4)
     te.wait_ge(s.lw, 32)
     for b in range(4):
+        te.wait_ge(s.qs, b + 1)
         te.matmul_mx(T.ps[:, 512 * b:512 * b + NC], T.cs[:, 128 * b:128 * b + 128], T.ss[:, 128 * b:128 * b + 128],
                      T.cw[:], T.sw[:], True, True).then_inc(s.pd, 1)
-    v.wait_ge(s.gsc, 1)
+    v.wait_ge(s.lg, 16)
     for b in range(4):
         v.wait_ge(s.pd, b + 1)
-        v.tensor_tensor(T.v[:, b:4 * NC:4], T.ps[:, 512 * b:512 * b + NC], T.gs[:, b:4 * NC:4],
+        v.tensor_tensor(T.v[:, b:4 * NC:4], T.ps[:, 512 * b:512 * b + NC], T.gin[:, b:4 * NC:4],
                         AluOpType.subtract).then_inc(s.sub, 1)
     v.wait_ge(s.sub, 4)
     v.quantize_mx(out=T.cg[:, NC * r:NC * r + NC], scales=T.sg[:, NC * r:NC * r + NC], in_=T.v[:]).then_inc(s.qv, 1)
     v.wait_ge(s.lx, 16)
     v.quantize_mx(out=T.cx[:], scales=T.sx[:], in_=T.xin[:]).then_inc(s.qx, 1)
 
-    m, feed = off_mask(core, T, topo), off_feed(core, T, topo)
+    m, feed = off_mask(core, T, topo), feed_mask(core, T, topo)
     g.wait_ge(s.qv, 1)
     n = 0
-    for kd in ("c", "s"):
-        hs = [helper_of(core, T, topo, side, k) for side, k, calls in HELPERS if any(q == kd for q, _ in calls)]
-        if hs:
-            n += send(g, T, topo, kd, r, hs, feed, s.fed)
-    for kd, offs in RANK_CALLS:
-        n += send(g, T, topo, kd, r, [T.cores[(r + d) % N] for d in offs], m, s["a%d" % r])
+    for what, kd, ts in RANK_CALLS:
+        if what == "feed":
+            n += send(g, T, topo, kd, r, [helper_of(core, T, topo, h) for h in ts], feed, s["fed" + kd])
+        else:
+            n += send(g, T, topo, kd, r, dests(r, ts, T, topo), m, s["a%d" % r])
 
     per = 2 * count(m)
 
     te.wait_ge(s.sub, 4)
     te.wait_ge(s.qv, 1)
     te.wait_ge(s.qx, 1)
-    order = [d for grp in GROUPS for d in grp]
-    nv, na = 0, 0
+    order = [r] + [j for t in ARRIVE for j in range(N) if j != r and dest(j, t, T, topo) == r]
     done = []
-    for i, d in enumerate(order):
-        b = (r - d) % N
-        if d:
+    for i, b in enumerate(order):
+        if b != r:
             te.wait_ge(s["a%d" % b], per)
         if i >= 8:
-            q, k = done[i - 8]
-            te.wait_ge(q, k)
+            te.wait_ge(*done[i - 8])
         bank = 512 * ((4 + i) % 8)
         te.matmul_mx(T.ps[:, bank:bank + NC], T.cg[:, NC * b:NC * b + NC], T.sg[:, NC * b:NC * b + NC],
                      T.cx[:], T.sx[:], True, True).then_inc(s.py, 1)
         dst, src = T.yb[:, NC * b:NC * b + NC], T.ps[:, bank:bank + NC]
         if i % 2 == 0:
             v.wait_ge(s.py, i + 1)
-            v.tensor_copy(dst, src).then_inc(s.cpv, 1)
-            nv += 1
-            done.append((s.cpv, nv))
+            v.tensor_scalar(dst, src, LR, None, AluOpType.mult).then_inc(s.cpv, 1)
+            done.append((s.cpv, i // 2 + 1))
         else:
             sc.wait_ge(s.py, i + 1)
-            sc.activation(dst, src, ActivationFunctionType.Copy).then_inc(s.cpa, 1)
-            na += 1
-            done.append((s.cpa, na))
-    i, st = 0, 0
-    for grp in GROUPS:
-        i += len(grp)
-        sy.wait_ge(s.cpv, (i + 1) // 2)
-        sy.wait_ge(s.cpa, i // 2)
-        for a, e in runs([(r - d) % N for d in grp]):
-            sy.dma_start(T.y[:, NC * a:NC * e], T.yb[:, NC * a:NC * e]).then_inc(s.st, 16)
-            st += 16
-    sy.wait_ge(s.st, st)
+            sc.activation(dst, src, ActivationFunctionType.Copy, scale=LR).then_inc(s.cpa, 1)
+            done.append((s.cpa, i // 2 + 1))
+        sy.wait_ge(*done[i])
+        sy.dma_start(T.y[:, NC * b:NC * b + NC], dst).then_inc(s.st, 16)
+    sy.wait_ge(s.st, 16 * N)
     g.wait_ge(s.sent, n)

from concourse.bass import DstId, RemoteDMATransfer
from concourse.mybir import dt, AluOpType, ActivationFunctionType

N, NC = 12, 128
ALL = 128
LR = 2.0 ** -3

HELPERS = [("far", 0, [("s", [2]), ("s", [6, 7]), ("c", [10])]),
           ("far", 1, [("s", [10]), ("s", [9, 4]), ("c", [7]), ("c", [0]), ("c", [1])]),
           ("near", 0, [("s", [0, 3, 1, 8]), ("c", [8]), ("c", [3])])]
RANK_CALLS = [("feed", "s", [0, 1, 2]), ("send", "c", [6, 9, 5]), ("send", "s", [5]),
              ("feed", "c", [0, 1]), ("feed", "c", [2]), ("send", "c", [2]), ("send", "c", [4])]
ARRIVE = [5, 6, 9, 2, 4, 10, 7, 0, 8, 1, 3]

SCRATCH = {
    "cw": ("sbuf", [128, NC], "float8_e4m3fn_x4"), "sw": ("sbuf", [128, NC], "uint8"),
    "gin": ("sbuf", [128, 4 * NC], "bfloat16"), "xin": ("sbuf", [128, 4 * NC], "bfloat16"),
    "cx": ("sbuf", [128, NC], "float8_e4m3fn_x4"), "sx": ("sbuf", [128, NC], "uint8"),
    "zero": ("sbuf", [128, 128], "bfloat16"), "eye": ("sbuf", [128, 516], "bfloat16"),
    "cs": ("sbuf", [128, 4 * 128], "float8_e4m3fn_x4"), "ss": ("sbuf", [128, 4 * 128], "uint8"),
    "v": ("sbuf", [128, 4 * NC], "bfloat16"),
    "cg": ("sbuf", [128, N * NC], "float8_e4m3fn_x4"), "sg": ("sbuf", [128, N * NC], "uint8"),
    "yb": ("sbuf", [128, N * NC], "float32"),
    "ps": ("psum", [128, 8 * 512], "float32"),
}
SEMAPHORES = (["lw", "lg", "lx", "fill", "rest", "eye1", "qs", "pd", "sub", "qv", "qx", "py", "cpv", "cpa", "st", "sent",
               "fedc", "feds"] + ["a%d" % j for j in range(N)])


def helper_of(core, T, topo, h):
    side, k, _ = HELPERS[h]
    same = [c for c in range(ALL) if topo.chip(c) == topo.chip(core) and T.rank_of(c) is None
            and (topo.die(c) == topo.die(core)) == (side == "near")
            and all(topo.may_write(c, d) for d in T.cores)]
    return same[k]


def dest(r, t, T, topo):
    ch = topo.chip(T.cores[r])
    own = [i for i in range(N) if i == r or topo.same_plane(topo.chip(T.cores[i]), ch)]
    other = [i for i in range(N) if i not in own]
    at = own.index(r)
    if t < len(own) - 1:
        return own[(at + 1 + t) % len(own)]
    return other[(at + t - (len(own) - 1)) % len(other)]


def dests(r, ts, T, topo):
    return [T.cores[dest(r, t, T, topo)] for t in ts]


def off_mask(core, T, topo):
    return min(topo.mask(core, d) for d in T.cores if topo.chip(d) != topo.chip(core))


def feed_mask(core, T, topo):
    here = [c for c in range(ALL) if topo.chip(c) == topo.chip(core) and c != core]
    return topo.mask(core, here[0]) & ~off_mask(core, T, topo)


def count(m):
    return bin(m).count("1")


def send(g, T, topo, kind, blk, dsts, mask, sem):
    ids = []
    for d in dsts:
        rid, pid, _ = topo.addr(d)
        ids.append(DstId(rid=rid, pnc=pid))
    a, b = blk * NC, (blk + 1) * NC
    ap = T.cg[:, a:b].bitcast(dt.uint8) if kind == "c" else T.sg[:, a:b]
    g.remote_dma_fused([RemoteDMATransfer(dst_ids=ids, dma_engine_mask=mask, remote_sem=sem,
                                          srcs=[ap], dsts=[ap for _ in dsts])], local_sem=T.sem.sent)
    return count(mask)


def helper_program(g, core, T, topo, r):
    for h in range(len(HELPERS)):
        if helper_of(T.cores[r], T, topo, h) != core:
            continue
        m, feed = off_mask(core, T, topo), feed_mask(T.cores[r], T, topo)
        n, seen = 0, []
        for kd, ts in HELPERS[h][2]:
            if kd not in seen:
                g.wait_ge(T.sem["fed" + kd], count(feed))
                seen.append(kd)
            n += send(g, T, topo, kd, r, dests(r, ts, T, topo), m, T.sem["a%d" % r])
        g.wait_ge(T.sem.sent, n)


def rank_program(g, core, T, topo):
    r = T.rank_of(core)
    if r is None:
        for j in range(N):
            if topo.chip(T.cores[j]) == topo.chip(core):
                helper_program(g, core, T, topo, j)
        return
    s = T.sem
    v, sc, te, sy = g.vector, g.scalar, g.tensor, g.sync

    sy.dma_start(T.cw[:].bitcast(dt.uint8), T.wc[:, :]).then_inc(s.lw, 16)
    sc.dma_start(T.sw[:], T.ws[:, :]).then_inc(s.lw, 16)
    sc.dma_start(T.gin[:], T.gr[:, :]).then_inc(s.lg, 16)
    sc.dma_start(T.xin[:], T.x[:, :]).then_inc(s.lx, 16)

    v.memset(T.zero[:], 0.0).then_inc(s.fill, 1)
    for k in range(3):
        v.memset(T.eye[:, k:516:4], 0.0).then_inc(s.rest, 1)
    g.wait_ge(s.fill, 1)
    g.affine_select(T.eye[:, 3:515:4], T.zero[:], [[-1, 128]], AluOpType.not_equal, 1.0 / LR, 0, 1).then_inc(s.eye1, 1)
    v.wait_ge(s.rest, 3)
    v.wait_ge(s.eye1, 1)
    for b in range(4):
        v.quantize_mx(out=T.cs[:, 128 * b:128 * b + 128], scales=T.ss[:, 128 * b:128 * b + 128],
                      in_=T.eye[:, 3 - b:515 - b]).then_inc(s.qs, 1)

    te.wait_ge(s.lw, 32)
    for b in range(4):
        te.wait_ge(s.qs, b + 1)
        te.matmul_mx(T.ps[:, 512 * b:512 * b + NC], T.cs[:, 128 * b:128 * b + 128], T.ss[:, 128 * b:128 * b + 128],
                     T.cw[:], T.sw[:], True, True).then_inc(s.pd, 1)
    v.wait_ge(s.lg, 16)
    for b in range(4):
        v.wait_ge(s.pd, b + 1)
        v.tensor_tensor(T.v[:, b:4 * NC:4], T.ps[:, 512 * b:512 * b + NC], T.gin[:, b:4 * NC:4],
                        AluOpType.subtract).then_inc(s.sub, 1)
    v.wait_ge(s.sub, 4)
    v.quantize_mx(out=T.cg[:, NC * r:NC * r + NC], scales=T.sg[:, NC * r:NC * r + NC], in_=T.v[:]).then_inc(s.qv, 1)
    v.wait_ge(s.lx, 16)
    v.quantize_mx(out=T.cx[:], scales=T.sx[:], in_=T.xin[:]).then_inc(s.qx, 1)

    m, feed = off_mask(core, T, topo), feed_mask(core, T, topo)
    g.wait_ge(s.qv, 1)
    n = 0
    for what, kd, ts in RANK_CALLS:
        if what == "feed":
            n += send(g, T, topo, kd, r, [helper_of(core, T, topo, h) for h in ts], feed, s["fed" + kd])
        else:
            n += send(g, T, topo, kd, r, dests(r, ts, T, topo), m, s["a%d" % r])

    per = 2 * count(m)

    te.wait_ge(s.sub, 4)
    te.wait_ge(s.qv, 1)
    te.wait_ge(s.qx, 1)
    order = [r] + [j for t in ARRIVE for j in range(N) if j != r and dest(j, t, T, topo) == r]
    done = []
    for i, b in enumerate(order):
        if b != r:
            te.wait_ge(s["a%d" % b], per)
        if i >= 8:
            te.wait_ge(*done[i - 8])
        bank = 512 * ((4 + i) % 8)
        te.matmul_mx(T.ps[:, bank:bank + NC], T.cg[:, NC * b:NC * b + NC], T.sg[:, NC * b:NC * b + NC],
                     T.cx[:], T.sx[:], True, True).then_inc(s.py, 1)
        dst, src = T.yb[:, NC * b:NC * b + NC], T.ps[:, bank:bank + NC]
        if i % 2 == 0:
            v.wait_ge(s.py, i + 1)
            v.tensor_scalar(dst, src, LR, None, AluOpType.mult).then_inc(s.cpv, 1)
            done.append((s.cpv, i // 2 + 1))
        else:
            sc.wait_ge(s.py, i + 1)
            sc.activation(dst, src, ActivationFunctionType.Copy, scale=LR).then_inc(s.cpa, 1)
            done.append((s.cpa, i // 2 + 1))
        sy.wait_ge(*done[i])
        sy.dma_start(T.y[:, NC * b:NC * b + NC], dst).then_inc(s.st, 16)
    sy.wait_ge(s.st, 16 * N)
    g.wait_ge(s.sent, n)
